import numpy as np
CORES = [0,1,2,3,4,5,6,7]
N = 8
H = 1
ROWS, COLS = 2, 4
PERIODIC = True
def setup_inputs(rng):
    return {"x": rng.standard_normal((N, 128, 4096), dtype=np.float32)}
def reference(x):
    W = x.shape[2]
    y = np.zeros((N, 4, 128, H), x.dtype)
    for r in range(N):
        i, j = divmod(r, COLS)
        for k, (di, dj, cols) in enumerate([(-1, 0, slice(W - H, W)), (1, 0, slice(0, H)), (0, -1, slice(W - H, W)), (0, 1, slice(0, H))]):
            a, b = i + di, j + dj
            if PERIODIC:
                a, b = a % ROWS, b % COLS
            if 0 <= a < ROWS and 0 <= b < COLS:
                y[r][k] = x[a * COLS + b][:, cols]
    return {"y": y}

@@ -1,0 +1,56 @@
+from concourse.bass import DstId, RemoteDMATransfer
+
+ROWS, COLS = 2, 4
+NORTH, SOUTH, WEST, EAST = 0, 1, 2, 3
+
+SCRATCH = {
+    "edge": ("sbuf", [128, 4], "float32"),
+    "land": ("dram", [4, 128, 1], "float32"),
+}
+SEMAPHORES = ["loaded", "moved", "stored"]
+
+LO_ENGINES = 0x00FF
+HI_ENGINES = 0xFF00
+
+
+def rank_program(g, core, T, topo):
+    rank = T.rank_of(core)
+    if rank is None:
+        return
+
+    i, j = divmod(rank, COLS)
+
+    def dst_id(di, dj):
+        c = T.cores[((i + di) % ROWS) * COLS + (j + dj) % COLS]
+        rid, pid, _se = topo.addr(c)
+        return DstId(rid=rid, pnc=pid)
+
+    W = T.x.shape[1]
+
+    g.sync.dma_start(T.edge[:, 0:2], T.x[:, 0:2]).then_inc(T.sem.loaded, 16)
+    g.scalar.dma_start(T.edge[:, 2:4], T.x[:, W - 2:W]).then_inc(T.sem.loaded, 16)
+    g.wait_ge(T.sem.loaded, 32)
+
+    g.remote_dma_fused(
+        [
+            RemoteDMATransfer(
+                dst_ids=[dst_id(-1, 0), dst_id(0, -1)],
+                dma_engine_mask=LO_ENGINES,
+                remote_sem=T.sem.moved,
+                srcs=[T.edge[:, 0:1]],
+                dsts=[T.land[SOUTH], T.land[EAST]],
+            ),
+            RemoteDMATransfer(
+                dst_ids=[dst_id(1, 0), dst_id(0, 1)],
+                dma_engine_mask=HI_ENGINES,
+                remote_sem=T.sem.moved,
+                srcs=[T.edge[:, 3:4]],
+                dsts=[T.land[NORTH], T.land[WEST]],
+            ),
+        ],
+        local_sem=T.sem.moved,
+    )
+
+    g.sync.wait_ge(T.sem.moved, 48)
+    g.sync.dma_start(T.y[:], T.land[:]).then_inc(T.sem.stored, 16)
+    g.sync.wait_ge(T.sem.stored, 16)

@@ -2,9 +2,10 @@ from concourse.bass import DstId, RemoteDMATransfer
 
 ROWS, COLS = 2, 4
 NORTH, SOUTH, WEST, EAST = 0, 1, 2, 3
+FIRST, LAST = 0, 1
 
 SCRATCH = {
-    "edge": ("sbuf", [128, 4], "float32"),
+    "edge": ("dram", [2, 128, 1], "float32"),
     "land": ("dram", [4, 128, 1], "float32"),
 }
 SEMAPHORES = ["loaded", "moved", "stored"]
@@ -27,8 +28,8 @@ def rank_program(g, core, T, topo):
 
     W = T.x.shape[1]
 
-    g.sync.dma_start(T.edge[:, 0:2], T.x[:, 0:2]).then_inc(T.sem.loaded, 16)
-    g.scalar.dma_start(T.edge[:, 2:4], T.x[:, W - 2:W]).then_inc(T.sem.loaded, 16)
+    g.dma_start(T.edge[FIRST], T.x[:, 0:1], allow_slow_non_contiguous=True).then_inc(T.sem.loaded, 16)
+    g.dma_start(T.edge[LAST], T.x[:, W - 1:W], allow_slow_non_contiguous=True).then_inc(T.sem.loaded, 16)
     g.wait_ge(T.sem.loaded, 32)
 
     g.remote_dma_fused(
@@ -37,14 +38,14 @@ def rank_program(g, core, T, topo):
                 dst_ids=[dst_id(-1, 0), dst_id(0, -1)],
                 dma_engine_mask=LO_ENGINES,
                 remote_sem=T.sem.moved,
-                srcs=[T.edge[:, 0:1]],
+                srcs=[T.edge[FIRST]],
                 dsts=[T.land[SOUTH], T.land[EAST]],
             ),
             RemoteDMATransfer(
                 dst_ids=[dst_id(1, 0), dst_id(0, 1)],
                 dma_engine_mask=HI_ENGINES,
                 remote_sem=T.sem.moved,
-                srcs=[T.edge[:, 3:4]],
+                srcs=[T.edge[LAST]],
                 dsts=[T.land[NORTH], T.land[WEST]],
             ),
         ],

from concourse.bass import DstId, RemoteDMATransfer

ROWS, COLS = 2, 4
NORTH, SOUTH, WEST, EAST = 0, 1, 2, 3
FIRST, LAST = 0, 1

SCRATCH = {
    "edge": ("dram", [2, 128, 1], "float32"),
    "land": ("dram", [4, 128, 1], "float32"),
}
SEMAPHORES = ["loaded", "moved", "stored"]

LO_ENGINES = 0x00FF
HI_ENGINES = 0xFF00


def rank_program(g, core, T, topo):
    rank = T.rank_of(core)
    if rank is None:
        return

    i, j = divmod(rank, COLS)

    def dst_id(di, dj):
        c = T.cores[((i + di) % ROWS) * COLS + (j + dj) % COLS]
        rid, pid, _se = topo.addr(c)
        return DstId(rid=rid, pnc=pid)

    W = T.x.shape[1]

    g.dma_start(T.edge[FIRST], T.x[:, 0:1], allow_slow_non_contiguous=True).then_inc(T.sem.loaded, 16)
    g.dma_start(T.edge[LAST], T.x[:, W - 1:W], allow_slow_non_contiguous=True).then_inc(T.sem.loaded, 16)
    g.wait_ge(T.sem.loaded, 32)

    g.remote_dma_fused(
        [
            RemoteDMATransfer(
                dst_ids=[dst_id(-1, 0), dst_id(0, -1)],
                dma_engine_mask=LO_ENGINES,
                remote_sem=T.sem.moved,
                srcs=[T.edge[FIRST]],
                dsts=[T.land[SOUTH], T.land[EAST]],
            ),
            RemoteDMATransfer(
                dst_ids=[dst_id(1, 0), dst_id(0, 1)],
                dma_engine_mask=HI_ENGINES,
                remote_sem=T.sem.moved,
                srcs=[T.edge[LAST]],
                dsts=[T.land[NORTH], T.land[WEST]],
            ),
        ],
        local_sem=T.sem.moved,
    )

    g.sync.wait_ge(T.sem.moved, 48)
    g.sync.dma_start(T.y[:], T.land[:]).then_inc(T.sem.stored, 16)
    g.sync.wait_ge(T.sem.stored, 16)
